import numpy as np
import ml_dtypes


def mxq(x, axis, fmt="e4m3"):
    dtype, down = {"e4m3": (ml_dtypes.float8_e4m3fn, 7), "e5m2": (ml_dtypes.float8_e5m2, 14)}[fmt]
    v = np.moveaxis(np.asarray(x, np.float32).astype(ml_dtypes.bfloat16).astype(np.float64), axis, -1)
    blocks = v.reshape(v.shape[:-1] + (-1, 32))
    amax = np.abs(blocks).max(-1, keepdims=True)
    byte = np.maximum(np.where(amax > 0, np.frexp(amax)[1] - 1 + 127, 0) - down, 1)
    scale = np.exp2(byte - 127.0)
    codes = (blocks / scale).astype(np.float32).astype(dtype).astype(np.float64)
    return np.moveaxis((codes * scale).reshape(v.shape), -1, axis)


WIDE = False


def mx_kscale(k):
    if not WIDE:
        return np.ones(k)
    levels = np.array([10, -10, 5, -5, 0])
    if k % 512:
        return np.exp2(np.random.permutation(np.resize(levels, k // 32))).repeat(32)
    a = np.empty((k // 512, 16))
    for p in range(k // 512):
        a[p, :8] = np.random.permutation(np.resize(levels, 8))
        for g in range(8):
            far = levels[np.abs(levels - a[p, g]) >= 10]
            a[p, g + 8] = far[np.random.randint(len(far))]
    return np.exp2(a.ravel()).repeat(32)


def f64(x):
    return np.asarray(x).astype(np.float64)


def striped(idx):
    return np.tile(idx.reshape(-1, 16).T, (8, 1)).astype(np.uint16)


def unstriped(offs):
    return offs[:16].T.reshape(-1).astype(np.int64)


def pack_weight(w):
    k, n = w.shape
    w = f64(np.asarray(w, np.float32).astype(ml_dtypes.bfloat16)).reshape(k // 32, 32, n)
    amax = np.abs(w).max(1)
    byte = np.clip(np.where(amax > 0, np.frexp(amax)[1] - 1 + 127 - 7, 1), 1, 254)
    scaled = (w * np.exp2(127.0 - byte)[:, None, :]).reshape(k, n).astype(np.float32)
    words = np.ascontiguousarray(scaled.reshape(k // 512, 128, 4, n).transpose(0, 1, 3, 2)).astype(ml_dtypes.float8_e4m3fn).view(np.uint8)
    return words, np.ascontiguousarray(byte.astype(np.uint8).reshape(k // 512, 16, n))


def unpack_weight(words, scales):
    g, p, n, _ = words.shape
    vals = np.ascontiguousarray(words).view(ml_dtypes.float8_e4m3fn).astype(np.float64) * np.repeat(np.exp2(scales.astype(np.float64) - 127.0), 8, axis=1)[..., None]
    return vals.transpose(0, 1, 3, 2).reshape(g * 512, n)


E2M1 = np.array([0.0, 0.5, 1.0, 1.5, 2.0, 3.0, 4.0, 6.0, -0.0, -0.5, -1.0, -1.5, -2.0, -3.0, -4.0, -6.0])


def pack_fp4(w):
    k, n = w.shape
    w = f64(np.asarray(w, np.float32).astype(ml_dtypes.bfloat16)).reshape(k // 32, 32, n)
    amax = np.abs(w).max(1)
    mant, ex = np.frexp(amax / 6.0)
    byte = np.clip(np.where(amax > 0, np.where(mant > 0.5, ex, ex - 1) + 127, 1), 1, 254)
    scaled = (w * np.exp2(127.0 - byte)[:, None, :]).reshape(k, n).astype(np.float32)
    c = np.ascontiguousarray(scaled.reshape(k // 512, 128, 4, n).transpose(0, 1, 3, 2)).astype(ml_dtypes.float4_e2m1fn).view(np.uint8) & 0xF
    words = (c[..., 0::2] | (c[..., 1::2] << 4)).reshape(k // 512, 128, 2 * n)
    return np.ascontiguousarray(words), np.ascontiguousarray(byte.astype(np.uint8).reshape(k // 512, 16, n))


def unpack_fp4(words, scales):
    g, _, n = scales.shape
    words = np.ascontiguousarray(words).reshape(g, 128, n, 2)
    nib = np.empty((g, 128, n, 4), np.uint8)
    nib[..., 0::2] = words & 0xF
    nib[..., 1::2] = words >> 4
    vals = E2M1[nib] * np.repeat(np.exp2(scales.astype(np.float64) - 127.0), 8, axis=1)[..., None]
    return vals.transpose(0, 1, 3, 2).reshape(g * 512, n)


def relu(v):
    return np.maximum(v, 0.0)


K, T, S, V, H, N = 512, 4096, 1024, 512, 512, 128


def setup_inputs():
    n = np.random.standard_normal
    s = mx_kscale(K)[:, None]
    u = mx_kscale(H)
    packed_xT = pack_weight(n((K, T)) * s)
    packed_w2 = pack_fp4(n((H, N)) / np.sqrt(2 * H) / u[:, None])
    packed_w3 = pack_fp4(n((H, N)) / np.sqrt(2 * H) / u[:, None])
    return {
        "x_words": packed_xT[0],
        "x_scales": packed_xT[1],
        "w1": (n((K, H)) / np.sqrt(K) / s * u).astype(np.float32),
        "w2_words": packed_w2[0],
        "w2_scales": packed_w2[1],
        "w3_words": packed_w3[0],
        "w3_scales": packed_w3[1],
        "offs": striped(np.random.permutation(T)[:S]),
        "cen": striped(np.random.permutation(S)[:V]),
        "pos1": striped(np.random.permutation(S)[:V]),
        "pos2": striped(np.random.permutation(S)[:V]),
        "pos3": striped(np.random.permutation(S)[:V]),
        "pos4": striped(np.random.permutation(S)[:V]),
    }


def reference(x_words, x_scales, w1, w2_words, w2_scales, w3_words, w3_scales, offs, cen, pos1, pos2, pos3, pos4):
    xq = unpack_weight(x_words, x_scales)[:, unstriped(offs)]
    h = relu(mxq(f64(w1), 0, "e4m3").T @ xq)
    hc = h[:, unstriped(cen)]
    z = np.maximum(np.maximum(np.maximum(h[:, unstriped(pos1)], h[:, unstriped(pos2)]), h[:, unstriped(pos3)]), h[:, unstriped(pos4)])
    return unpack_fp4(w2_words, w2_scales).T @ mxq(hc, 0, "e4m3") + unpack_fp4(w3_words, w3_scales).T @ mxq(z, 0, "e4m3")

@@ -1,0 +1,183 @@
+from contextlib import ExitStack
+
+import concourse.mybir as mybir
+
+K, T, S, V, H, N = 512, 4096, 1024, 512, 512, 128
+FLOPS = 2 * K * H * S + 2 * 2 * H * N * V
+
+F32 = mybir.dt.float32
+BF16 = mybir.dt.bfloat16
+I32 = mybir.dt.int32
+U32 = mybir.dt.uint32
+U16 = mybir.dt.uint16
+U8 = mybir.dt.uint8
+FP8X4 = mybir.dt.float8_e4m3fn_x4
+FP4X4 = mybir.dt.float4_e2m1fn_x4
+ACT = mybir.ActivationFunctionType
+MAX = mybir.AluOpType.max
+
+P = 128
+PACK = 4
+BANK = 512
+GROUP = 128
+
+
+def tile_picked_sagecat_max_p_kernel(
+    tc, x_words, x_scales, w1, w2_words, w2_scales, w3_words, w3_scales, offs, cen, pos1, pos2, pos3, pos4, out
+):
+    nc = tc.nc
+    with ExitStack() as ctx:
+        lists = ctx.enter_context(tc.tile_pool(name="lists", bufs=1))
+        sb = ctx.enter_context(tc.tile_pool(name="sb", bufs=1))
+        psum = ctx.enter_context(tc.psum_pool(name="psum", bufs=8))
+
+        def load_list(name, src, entries):
+            t = lists.tile([P, entries // 16], U16, name=name)
+            nc.sync.dma_start(t[:], src)
+            return t
+
+        def load_scale_rows(queue, dst, src):
+            for q in range(4):
+                queue.dma_start(dst[32 * q : 32 * q + 4, :].bitcast(I32), src[4 * q : 4 * q + 4, :].bitcast(I32))
+
+        xs = sb.tile([P, T], U8, name="xs", align_bytes=64)
+        nc.vector.memset(xs[:].bitcast(I32), 0)
+        offs_t = load_list("offs_t", offs, S)
+        w1_rows = w1.rearrange("(p j) c -> p j c", j=PACK)
+        w1_raw = []
+
+        def load_w1(c0, c1):
+            r = sb.tile([P, PACK, c1 - c0], F32, name=f"w1_raw{c0}", align_bytes=64)
+            nc.sync.dma_start(r[:], w1_rows[:, :, c0:c1])
+            w1_raw.append((c0, c1, r))
+
+        load_w1(0, 256)
+        load_scale_rows(nc.sync, xs, x_scales[0])
+        xw = sb.tile([P, T], U32, name="xw", align_bytes=64)
+        nc.sync.dma_start(xw[:].bitcast(I32), x_words[0].rearrange("p n t -> p (n t)").bitcast(I32))
+        load_w1(256, 384)
+        load_w1(384, 512)
+        pos_t = [load_list(f"pos{d}_t", src, V) for d, src in enumerate((pos1, pos2, pos3, pos4))]
+        cen_t = load_list("cen_t", cen, V)
+        w2w = sb.tile([P, 2 * N], U8, name="w2w", align_bytes=64)
+        w3w = sb.tile([P, 2 * N], U8, name="w3w", align_bytes=64)
+        nc.sync.dma_start(w3w[:].bitcast(I32), w3_words[0].bitcast(I32))
+        nc.sync.dma_start(w2w[:].bitcast(I32), w2_words[0].bitcast(I32))
+        w2s = sb.tile([P, N], U8, name="w2s", align_bytes=64)
+        w3s = sb.tile([P, N], U8, name="w3s", align_bytes=64)
+        nc.vector.memset(w3s[:].bitcast(I32), 0)
+        nc.vector.memset(w2s[:].bitcast(I32), 0)
+        load_scale_rows(nc.sync, w3s, w3_scales[0])
+        load_scale_rows(nc.sync, w2s, w2_scales[0])
+
+        gs = sb.tile([P, S], U8, name="gs", align_bytes=64)
+        gw = sb.tile([P, S], U32, name="gw", align_bytes=64)
+        nc.vector.tensor_copy(gs[:], xs[:].indirect(offs_t[:]))
+        nc.vector.tensor_copy(gw[:], xw[:].indirect(offs_t[:]))
+
+        wg = sb.tile([P, PACK * H], BF16, name="wg", align_bytes=64)
+        wg_v = wg[:].rearrange("p (t m j) -> p m j t", t=PACK, j=PACK)
+        for c0, c1, r in w1_raw:
+            nc.scalar.activation(wg_v[:, c0 // PACK : c1 // PACK], r[:].rearrange("p j (m t) -> p m j t", t=PACK), ACT.Copy)
+        w1c = sb.tile([P, H], U32, name="w1c", align_bytes=64)
+        w1s = sb.tile([P, H], U8, name="w1s", align_bytes=64)
+        nc.vector.quantize_mx(out=w1c[:, 0:P].bitcast(FP8X4), scales=w1s[:, 0:P], in_=wg[:, 0 : PACK * P])
+        nc.vector.quantize_mx(out=w1c[:, P : 2 * P].bitcast(FP8X4), scales=w1s[:, P : 2 * P], in_=wg[:, PACK * P : 2 * PACK * P])
+        nc.vector.quantize_mx(out=w1c[:, 2 * P : 4 * P].bitcast(FP8X4), scales=w1s[:, 2 * P : 4 * P], in_=wg[:, 2 * PACK * P : 4 * PACK * P])
+
+        h = []
+        for t in range(PACK):
+            ht = sb.tile([P, S], F32, name=f"h{t}", align_bytes=64)
+            width = BANK // 2 if t == 0 else BANK
+            for b in range(S // width):
+                cols = slice(b * width, (b + 1) * width)
+                acc = psum.tile([P, width], F32, name="acc", tag="bank")
+                nc.tensor.matmul_mx(
+                    out=acc[:],
+                    lhsT=w1c[:, t * P : (t + 1) * P].bitcast(FP8X4),
+                    lhsT_scale=w1s[:, t * P : (t + 1) * P],
+                    rhs=gw[:, cols].bitcast(FP8X4),
+                    rhs_scale=gs[:, cols],
+                    start=True,
+                    stop=True,
+                )
+                if t == 0 and b % 2 == 1:
+                    nc.vector.tensor_scalar_max(ht[:, cols], acc[:], 0.0)
+                else:
+                    nc.scalar.activation(ht[:, cols], acc[:], ACT.Relu)
+            h.append(ht)
+
+        nb = [sb.tile([P, PACK, V], BF16, name=f"nb{d}", align_bytes=64) for d in range(4)]
+        for t in range(PACK):
+            for d in range(4):
+                nc.vector.tensor_copy(nb[d][:, t, :], h[t][:].indirect(pos_t[d][:]))
+        m01 = sb.tile([P, PACK, V], BF16, name="m01", align_bytes=64)
+        m23 = sb.tile([P, PACK, V], BF16, name="m23", align_bytes=64)
+        nc.vector.tensor_tensor(m01[:], nb[0][:], nb[1][:], MAX)
+        nc.vector.tensor_tensor(m23[:], nb[2][:], nb[3][:], MAX)
+
+        def interleave(dst, src):
+            nc.scalar.copy(
+                dst[:].rearrange("p (c i t) -> p c t i", i=4, t=PACK), src[:].rearrange("p t (c i) -> p c t i", i=4)
+            )
+
+        def gather_cen(dst, t, v0, v1):
+            nc.vector.tensor_copy(dst, h[t][:].indirect(cen_t[:, v0 // 16 : v1 // 16]))
+
+        zc = sb.tile([P, V], U32, name="zc", align_bytes=64)
+        zs = sb.tile([P, V], U8, name="zs", align_bytes=64)
+        cc = sb.tile([P, V], U32, name="cc", align_bytes=64)
+        cs = sb.tile([P, V], U8, name="cs", align_bytes=64)
+
+        def quant(codes, scales, v0, v1, src):
+            nc.vector.quantize_mx(out=codes[:, v0:v1].bitcast(FP8X4), scales=scales[:, v0:v1], in_=src[:])
+
+        cA = sb.tile([P, PACK, 256], BF16, name="cA", tag="nb0", align_bytes=64)
+        gather_cen(cA[:, 0, :], 0, 0, 256)
+        zp, zi = [], []
+        for u in range(2):
+            z = sb.tile([P, PACK, 256], BF16, name=f"zp{u}", align_bytes=64)
+            nc.vector.tensor_tensor(z[:], m01[:, :, u * 256 : (u + 1) * 256], m23[:, :, u * 256 : (u + 1) * 256], MAX)
+            i = sb.tile([P, PACK * 256], BF16, name=f"zi{u}", align_bytes=64)
+            interleave(i, z)
+            zp.append(z)
+            zi.append(i)
+        for t in range(1, PACK):
+            gather_cen(cA[:, t, :], t, 0, 256)
+        iA = sb.tile([P, PACK * 256], BF16, name="iA", align_bytes=64)
+        interleave(iA, cA)
+        quant(zc, zs, 0, 256, zi[0])
+        quant(zc, zs, 256, 512, zi[1])
+        cB = sb.tile([P, PACK, 128], BF16, name="cB", tag="zp1", align_bytes=64)
+        for t in range(PACK):
+            gather_cen(cB[:, t, :], t, 256, 384)
+        iB = sb.tile([P, PACK * 128], BF16, name="iB", align_bytes=64)
+        interleave(iB, cB)
+        quant(cc, cs, 0, 256, iA)
+        iC = sb.tile([P, PACK * 128], BF16, name="iC", tag="iA", align_bytes=64)
+        iC_v = iC[:].rearrange("p (v t) -> p t v", t=PACK)
+        for t in range(PACK):
+            gather_cen(iC_v[:, t, :], t, 384, 512)
+        quant(cc, cs, 256, 384, iB)
+        quant(cc, cs, 384, 512, iC)
+
+        accs = [psum.tile([P, GROUP], F32, name=f"o{g}", tag="bank") for g in range(V // GROUP)]
+        for g in range(V // GROUP):
+            cols = slice(g * GROUP, (g + 1) * GROUP)
+            nc.tensor.matmul_mx(
+                out=accs[g][:], lhsT=w3w[:].bitcast(FP4X4), lhsT_scale=w3s[:],
+                rhs=zc[:, cols].bitcast(FP8X4), rhs_scale=zs[:, cols], start=True, stop=False,
+            )
+        res = [sb.tile([P, w], F32, name=f"res{n}", align_bytes=64) for n, w in enumerate((256, 128, 128))]
+        place = ((0, 0), (0, 128), (1, 0), (2, 0))
+        for g in range(V // GROUP):
+            cols = slice(g * GROUP, (g + 1) * GROUP)
+            nc.tensor.matmul_mx(
+                out=accs[g][:], lhsT=w2w[:].bitcast(FP4X4), lhsT_scale=w2s[:],
+                rhs=cc[:, cols].bitcast(FP8X4), rhs_scale=cs[:, cols], start=False, stop=True,
+            )
+            n, c0 = place[g]
+            nc.scalar.copy(res[n][:, c0 : c0 + GROUP], accs[g][:])
+            if g >= 1:
+                v0 = (0, 256, 384)[n]
+                nc.sync.dma_start(out[:, v0 : (g + 1) * GROUP], res[n][:])

@@ -20,6 +20,7 @@ P = 128
 PACK = 4
 BANK = 512
 GROUP = 128
+X_HEAD = T // 8
 
 
 def tile_picked_sagecat_max_p_kernel(
@@ -37,8 +38,8 @@ def tile_picked_sagecat_max_p_kernel(
             return t
 
         def load_scale_rows(queue, dst, src):
-            for q in range(4):
-                queue.dma_start(dst[32 * q : 32 * q + 4, :].bitcast(I32), src[4 * q : 4 * q + 4, :].bitcast(I32))
+            for r in range(4):
+                queue.dma_start(dst[r:P:32, :].bitcast(I32), src[r:16:4, :].bitcast(I32))
 
         xs = sb.tile([P, T], U8, name="xs", align_bytes=64)
         nc.vector.memset(xs[:].bitcast(I32), 0)
@@ -51,10 +52,13 @@ def tile_picked_sagecat_max_p_kernel(
             nc.sync.dma_start(r[:], w1_rows[:, :, c0:c1])
             w1_raw.append((c0, c1, r))
 
-        load_w1(0, 256)
-        load_scale_rows(nc.sync, xs, x_scales[0])
         xw = sb.tile([P, T], U32, name="xw", align_bytes=64)
-        nc.sync.dma_start(xw[:].bitcast(I32), x_words[0].rearrange("p n t -> p (n t)").bitcast(I32))
+        xw_hbm = x_words[0].rearrange("p n t -> p (n t)").bitcast(I32)
+        load_w1(0, 128)
+        nc.sync.dma_start(xw[:, 0:X_HEAD].bitcast(I32), xw_hbm[:, 0:X_HEAD])
+        nc.sync.dma_start(xs[0:P:8, :].bitcast(I32), x_scales[0].bitcast(I32))
+        nc.sync.dma_start(xw[:, X_HEAD:T].bitcast(I32), xw_hbm[:, X_HEAD:T])
+        load_w1(128, 256)
         load_w1(256, 384)
         load_w1(384, 512)
         pos_t = [load_list(f"pos{d}_t", src, V) for d, src in enumerate((pos1, pos2, pos3, pos4))]
@@ -72,13 +76,18 @@ def tile_picked_sagecat_max_p_kernel(
 
         gs = sb.tile([P, S], U8, name="gs", align_bytes=64)
         gw = sb.tile([P, S], U32, name="gw", align_bytes=64)
-        nc.vector.tensor_copy(gs[:], xs[:].indirect(offs_t[:]))
+        gs_raw = sb.tile([P, S], U8, name="gs_raw", align_bytes=64)
+        nc.vector.memset(gs[:].bitcast(I32), 0)
+        nc.vector.tensor_copy(gs_raw[:], xs[:].indirect(offs_t[:]))
+        for r in range(4):
+            nc.scalar.dma_start(gs[r:P:32, :].bitcast(I32), gs_raw[8 * r : P : 32, :].bitcast(I32))
         nc.vector.tensor_copy(gw[:], xw[:].indirect(offs_t[:]))
 
         wg = sb.tile([P, PACK * H], BF16, name="wg", align_bytes=64)
         wg_v = wg[:].rearrange("p (t m j) -> p m j t", t=PACK, j=PACK)
         for c0, c1, r in w1_raw:
-            nc.scalar.activation(wg_v[:, c0 // PACK : c1 // PACK], r[:].rearrange("p j (m t) -> p m j t", t=PACK), ACT.Copy)
+            dst, src = wg_v[:, c0 // PACK : c1 // PACK], r[:].rearrange("p j (m t) -> p m j t", t=PACK)
+            nc.scalar.activation(dst, src, ACT.Copy)
         w1c = sb.tile([P, H], U32, name="w1c", align_bytes=64)
         w1s = sb.tile([P, H], U8, name="w1s", align_bytes=64)
         nc.vector.quantize_mx(out=w1c[:, 0:P].bitcast(FP8X4), scales=w1s[:, 0:P], in_=wg[:, 0 : PACK * P])
@@ -118,7 +127,7 @@ def tile_picked_sagecat_max_p_kernel(
 
         def interleave(dst, src):
             nc.scalar.copy(
-                dst[:].rearrange("p (c i t) -> p c t i", i=4, t=PACK), src[:].rearrange("p t (c i) -> p c t i", i=4)
+                dst.rearrange("p (c i t) -> p c t i", i=4, t=PACK), src[:].rearrange("p t (c i) -> p c t i", i=4)
             )
 
         def gather_cen(dst, t, v0, v1):
@@ -134,27 +143,23 @@ def tile_picked_sagecat_max_p_kernel(
 
         cA = sb.tile([P, PACK, 256], BF16, name="cA", tag="nb0", align_bytes=64)
         gather_cen(cA[:, 0, :], 0, 0, 256)
-        zp, zi = [], []
+        zi = sb.tile([P, PACK * V], BF16, name="zi", align_bytes=64)
         for u in range(2):
             z = sb.tile([P, PACK, 256], BF16, name=f"zp{u}", align_bytes=64)
             nc.vector.tensor_tensor(z[:], m01[:, :, u * 256 : (u + 1) * 256], m23[:, :, u * 256 : (u + 1) * 256], MAX)
-            i = sb.tile([P, PACK * 256], BF16, name=f"zi{u}", align_bytes=64)
-            interleave(i, z)
-            zp.append(z)
-            zi.append(i)
+            interleave(zi[:, u * PACK * 256 : (u + 1) * PACK * 256], z)
         for t in range(1, PACK):
             gather_cen(cA[:, t, :], t, 0, 256)
         iA = sb.tile([P, PACK * 256], BF16, name="iA", align_bytes=64)
-        interleave(iA, cA)
-        quant(zc, zs, 0, 256, zi[0])
-        quant(zc, zs, 256, 512, zi[1])
-        cB = sb.tile([P, PACK, 128], BF16, name="cB", tag="zp1", align_bytes=64)
+        interleave(iA[:], cA)
+        cB = sb.tile([P, PACK, 128], BF16, name="cB", tag="nb1", align_bytes=64)
         for t in range(PACK):
             gather_cen(cB[:, t, :], t, 256, 384)
         iB = sb.tile([P, PACK * 128], BF16, name="iB", align_bytes=64)
-        interleave(iB, cB)
+        interleave(iB[:], cB)
+        quant(zc, zs, 0, 512, zi)
         quant(cc, cs, 0, 256, iA)
-        iC = sb.tile([P, PACK * 128], BF16, name="iC", tag="iA", align_bytes=64)
+        iC = sb.tile([P, PACK * 128], BF16, name="iC", tag="nb0", align_bytes=64)
         iC_v = iC[:].rearrange("p (v t) -> p t v", t=PACK)
         for t in range(PACK):
             gather_cen(iC_v[:, t, :], t, 384, 512)
@@ -177,7 +182,11 @@ def tile_picked_sagecat_max_p_kernel(
                 rhs=cc[:, cols].bitcast(FP8X4), rhs_scale=cs[:, cols], start=False, stop=True,
             )
             n, c0 = place[g]
-            nc.scalar.copy(res[n][:, c0 : c0 + GROUP], accs[g][:])
+            if g == 3:
+                nc.vector.tensor_copy(res[n][:, c0 : c0 + GROUP], accs[g][:])
+            else:
+                nc.scalar.copy(res[n][:, c0 : c0 + GROUP], accs[g][:])
             if g >= 1:
                 v0 = (0, 256, 384)[n]
-                nc.sync.dma_start(out[:, v0 : (g + 1) * GROUP], res[n][:])
+                queue = nc.scalar if g == 2 else nc.sync
+                queue.dma_start(out[:, v0 : (g + 1) * GROUP], res[n][:])

@@ -20,7 +20,7 @@ P = 128
 PACK = 4
 BANK = 512
 GROUP = 128
-X_HEAD = T // 8
+X_HEAD = T // 4
 
 
 def tile_picked_sagecat_max_p_kernel(
@@ -54,13 +54,10 @@ def tile_picked_sagecat_max_p_kernel(
 
         xw = sb.tile([P, T], U32, name="xw", align_bytes=64)
         xw_hbm = x_words[0].rearrange("p n t -> p (n t)").bitcast(I32)
-        load_w1(0, 128)
         nc.sync.dma_start(xw[:, 0:X_HEAD].bitcast(I32), xw_hbm[:, 0:X_HEAD])
         nc.sync.dma_start(xs[0:P:8, :].bitcast(I32), x_scales[0].bitcast(I32))
         nc.sync.dma_start(xw[:, X_HEAD:T].bitcast(I32), xw_hbm[:, X_HEAD:T])
-        load_w1(128, 256)
-        load_w1(256, 384)
-        load_w1(384, 512)
+        load_w1(0, 512)
         pos_t = [load_list(f"pos{d}_t", src, V) for d, src in enumerate((pos1, pos2, pos3, pos4))]
         cen_t = load_list("cen_t", cen, V)
         w2w = sb.tile([P, 2 * N], U8, name="w2w", align_bytes=64)
@@ -85,9 +82,9 @@ def tile_picked_sagecat_max_p_kernel(
 
         wg = sb.tile([P, PACK * H], BF16, name="wg", align_bytes=64)
         wg_v = wg[:].rearrange("p (t m j) -> p m j t", t=PACK, j=PACK)
-        for c0, c1, r in w1_raw:
-            dst, src = wg_v[:, c0 // PACK : c1 // PACK], r[:].rearrange("p j (m t) -> p m j t", t=PACK)
-            nc.scalar.activation(dst, src, ACT.Copy)
+        w1_v = w1_raw[0][2][:].rearrange("p j (m t) -> p m j t", t=PACK)
+        nc.scalar.activation(wg_v[:, 0:40], w1_v[:, 0:40], ACT.Copy)
+        nc.vector.tensor_copy(wg_v[:, 40:P], w1_v[:, 40:P])
         w1c = sb.tile([P, H], U32, name="w1c", align_bytes=64)
         w1s = sb.tile([P, H], U8, name="w1s", align_bytes=64)
         nc.vector.quantize_mx(out=w1c[:, 0:P].bitcast(FP8X4), scales=w1s[:, 0:P], in_=wg[:, 0 : PACK * P])

@@ -43,21 +43,14 @@ def tile_picked_sagecat_max_p_kernel(
 
         xs = sb.tile([P, T], U8, name="xs", align_bytes=64)
         nc.vector.memset(xs[:].bitcast(I32), 0)
-        offs_t = load_list("offs_t", offs, S)
         w1_rows = w1.rearrange("(p j) c -> p j c", j=PACK)
-        w1_raw = []
-
-        def load_w1(c0, c1):
-            r = sb.tile([P, PACK, c1 - c0], F32, name=f"w1_raw{c0}", align_bytes=64)
-            nc.sync.dma_start(r[:], w1_rows[:, :, c0:c1])
-            w1_raw.append((c0, c1, r))
-
-        xw = sb.tile([P, T], U32, name="xw", align_bytes=64)
-        xw_hbm = x_words[0].rearrange("p n t -> p (n t)").bitcast(I32)
-        nc.sync.dma_start(xw[:, 0:X_HEAD].bitcast(I32), xw_hbm[:, 0:X_HEAD])
+        w1_raw = sb.tile([P, PACK, H], F32, name="w1_raw", align_bytes=64)
+        nc.sync.dma_start(w1_raw[:, 0:2, :], w1_rows[:, 0:2, :])
         nc.sync.dma_start(xs[0:P:8, :].bitcast(I32), x_scales[0].bitcast(I32))
-        nc.sync.dma_start(xw[:, X_HEAD:T].bitcast(I32), xw_hbm[:, X_HEAD:T])
-        load_w1(0, 512)
+        offs_t = load_list("offs_t", offs, S)
+        nc.sync.dma_start(w1_raw[:, 2:4, :], w1_rows[:, 2:4, :])
+        xw = sb.tile([P, T], U32, name="xw", align_bytes=64)
+        nc.sync.dma_start(xw[:].bitcast(I32), x_words[0].rearrange("p n t -> p (n t)").bitcast(I32))
         pos_t = [load_list(f"pos{d}_t", src, V) for d, src in enumerate((pos1, pos2, pos3, pos4))]
         cen_t = load_list("cen_t", cen, V)
         w2w = sb.tile([P, 2 * N], U8, name="w2w", align_bytes=64)
@@ -78,26 +71,23 @@ def tile_picked_sagecat_max_p_kernel(
         nc.vector.tensor_copy(gs_raw[:], xs[:].indirect(offs_t[:]))
         for r in range(4):
             nc.scalar.dma_start(gs[r:P:32, :].bitcast(I32), gs_raw[8 * r : P : 32, :].bitcast(I32))
-        nc.vector.tensor_copy(gw[:], xw[:].indirect(offs_t[:]))
 
         wg = sb.tile([P, PACK * H], BF16, name="wg", align_bytes=64)
         wg_v = wg[:].rearrange("p (t m j) -> p m j t", t=PACK, j=PACK)
-        w1_v = w1_raw[0][2][:].rearrange("p j (m t) -> p m j t", t=PACK)
-        nc.scalar.activation(wg_v[:, 0:40], w1_v[:, 0:40], ACT.Copy)
-        nc.vector.tensor_copy(wg_v[:, 40:P], w1_v[:, 40:P])
+        nc.vector.tensor_copy(wg_v, w1_raw[:].rearrange("p j (m t) -> p m j t", t=PACK))
         w1c = sb.tile([P, H], U32, name="w1c", align_bytes=64)
         w1s = sb.tile([P, H], U8, name="w1s", align_bytes=64)
-        nc.vector.quantize_mx(out=w1c[:, 0:P].bitcast(FP8X4), scales=w1s[:, 0:P], in_=wg[:, 0 : PACK * P])
-        nc.vector.quantize_mx(out=w1c[:, P : 2 * P].bitcast(FP8X4), scales=w1s[:, P : 2 * P], in_=wg[:, PACK * P : 2 * PACK * P])
-        nc.vector.quantize_mx(out=w1c[:, 2 * P : 4 * P].bitcast(FP8X4), scales=w1s[:, 2 * P : 4 * P], in_=wg[:, 2 * PACK * P : 4 * PACK * P])
+        nc.vector.quantize_mx(out=w1c[:].bitcast(FP8X4), scales=w1s[:], in_=wg[:])
+        for b in range(S // BANK):
+            nc.vector.tensor_copy(gw[:, b * BANK : (b + 1) * BANK], xw[:].indirect(offs_t[:, b * BANK // 16 : (b + 1) * BANK // 16]))
 
         h = []
         for t in range(PACK):
             ht = sb.tile([P, S], F32, name=f"h{t}", align_bytes=64)
-            width = BANK // 2 if t == 0 else BANK
-            for b in range(S // width):
-                cols = slice(b * width, (b + 1) * width)
-                acc = psum.tile([P, width], F32, name="acc", tag="bank")
+            edges = (0, 512, 768, 1024) if t == 0 else (0, 512, 1024)
+            for b in range(len(edges) - 1):
+                cols = slice(edges[b], edges[b + 1])
+                acc = psum.tile([P, edges[b + 1] - edges[b]], F32, name="acc", tag="bank")
                 nc.tensor.matmul_mx(
                     out=acc[:],
                     lhsT=w1c[:, t * P : (t + 1) * P].bitcast(FP8X4),
@@ -107,7 +97,7 @@ def tile_picked_sagecat_max_p_kernel(
                     start=True,
                     stop=True,
                 )
-                if t == 0 and b % 2 == 1:
+                if b == 2:
                     nc.vector.tensor_scalar_max(ht[:, cols], acc[:], 0.0)
                 else:
                     nc.scalar.activation(ht[:, cols], acc[:], ACT.Relu)
@@ -158,7 +148,11 @@ def tile_picked_sagecat_max_p_kernel(
         quant(cc, cs, 0, 256, iA)
         iC = sb.tile([P, PACK * 128], BF16, name="iC", tag="nb0", align_bytes=64)
         iC_v = iC[:].rearrange("p (v t) -> p t v", t=PACK)
-        for t in range(PACK):
+        cC = sb.tile([P, 2, 128], BF16, name="cC", tag="zp1", align_bytes=64)
+        for t in range(2):
+            gather_cen(cC[:, t, :], t, 384, 512)
+        nc.scalar.copy(iC[:].rearrange("p (v t) -> p v t", t=PACK)[:, :, 0:2], cC[:].rearrange("p t v -> p v t"))
+        for t in range(2, PACK):
             gather_cen(iC_v[:, t, :], t, 384, 512)
         quant(cc, cs, 256, 384, iB)
         quant(cc, cs, 384, 512, iC)

from contextlib import ExitStack

import concourse.mybir as mybir

K, T, S, V, H, N = 512, 4096, 1024, 512, 512, 128
FLOPS = 2 * K * H * S + 2 * 2 * H * N * V

F32 = mybir.dt.float32
BF16 = mybir.dt.bfloat16
I32 = mybir.dt.int32
U32 = mybir.dt.uint32
U16 = mybir.dt.uint16
U8 = mybir.dt.uint8
FP8X4 = mybir.dt.float8_e4m3fn_x4
FP4X4 = mybir.dt.float4_e2m1fn_x4
ACT = mybir.ActivationFunctionType
MAX = mybir.AluOpType.max

P = 128
PACK = 4
BANK = 512
GROUP = 128
X_HEAD = T // 4


def tile_picked_sagecat_max_p_kernel(
    tc, x_words, x_scales, w1, w2_words, w2_scales, w3_words, w3_scales, offs, cen, pos1, pos2, pos3, pos4, out
):
    nc = tc.nc
    with ExitStack() as ctx:
        lists = ctx.enter_context(tc.tile_pool(name="lists", bufs=1))
        sb = ctx.enter_context(tc.tile_pool(name="sb", bufs=1))
        psum = ctx.enter_context(tc.psum_pool(name="psum", bufs=8))

        def load_list(name, src, entries):
            t = lists.tile([P, entries // 16], U16, name=name)
            nc.sync.dma_start(t[:], src)
            return t

        def load_scale_rows(queue, dst, src):
            for r in range(4):
                queue.dma_start(dst[r:P:32, :].bitcast(I32), src[r:16:4, :].bitcast(I32))

        xs = sb.tile([P, T], U8, name="xs", align_bytes=64)
        nc.vector.memset(xs[:].bitcast(I32), 0)
        w1_rows = w1.rearrange("(p j) c -> p j c", j=PACK)
        w1_raw = sb.tile([P, PACK, H], F32, name="w1_raw", align_bytes=64)
        nc.sync.dma_start(w1_raw[:, 0:2, :], w1_rows[:, 0:2, :])
        nc.sync.dma_start(xs[0:P:8, :].bitcast(I32), x_scales[0].bitcast(I32))
        offs_t = load_list("offs_t", offs, S)
        nc.sync.dma_start(w1_raw[:, 2:4, :], w1_rows[:, 2:4, :])
        xw = sb.tile([P, T], U32, name="xw", align_bytes=64)
        nc.sync.dma_start(xw[:].bitcast(I32), x_words[0].rearrange("p n t -> p (n t)").bitcast(I32))
        pos_t = [load_list(f"pos{d}_t", src, V) for d, src in enumerate((pos1, pos2, pos3, pos4))]
        cen_t = load_list("cen_t", cen, V)
        w2w = sb.tile([P, 2 * N], U8, name="w2w", align_bytes=64)
        w3w = sb.tile([P, 2 * N], U8, name="w3w", align_bytes=64)
        nc.sync.dma_start(w3w[:].bitcast(I32), w3_words[0].bitcast(I32))
        nc.sync.dma_start(w2w[:].bitcast(I32), w2_words[0].bitcast(I32))
        w2s = sb.tile([P, N], U8, name="w2s", align_bytes=64)
        w3s = sb.tile([P, N], U8, name="w3s", align_bytes=64)
        nc.vector.memset(w3s[:].bitcast(I32), 0)
        nc.vector.memset(w2s[:].bitcast(I32), 0)
        load_scale_rows(nc.sync, w3s, w3_scales[0])
        load_scale_rows(nc.sync, w2s, w2_scales[0])

        gs = sb.tile([P, S], U8, name="gs", align_bytes=64)
        gw = sb.tile([P, S], U32, name="gw", align_bytes=64)
        gs_raw = sb.tile([P, S], U8, name="gs_raw", align_bytes=64)
        nc.vector.memset(gs[:].bitcast(I32), 0)
        nc.vector.tensor_copy(gs_raw[:], xs[:].indirect(offs_t[:]))
        for r in range(4):
            nc.scalar.dma_start(gs[r:P:32, :].bitcast(I32), gs_raw[8 * r : P : 32, :].bitcast(I32))

        wg = sb.tile([P, PACK * H], BF16, name="wg", align_bytes=64)
        wg_v = wg[:].rearrange("p (t m j) -> p m j t", t=PACK, j=PACK)
        nc.vector.tensor_copy(wg_v, w1_raw[:].rearrange("p j (m t) -> p m j t", t=PACK))
        w1c = sb.tile([P, H], U32, name="w1c", align_bytes=64)
        w1s = sb.tile([P, H], U8, name="w1s", align_bytes=64)
        nc.vector.quantize_mx(out=w1c[:].bitcast(FP8X4), scales=w1s[:], in_=wg[:])
        for b in range(S // BANK):
            nc.vector.tensor_copy(gw[:, b * BANK : (b + 1) * BANK], xw[:].indirect(offs_t[:, b * BANK // 16 : (b + 1) * BANK // 16]))

        h = []
        for t in range(PACK):
            ht = sb.tile([P, S], F32, name=f"h{t}", align_bytes=64)
            edges = (0, 512, 768, 1024) if t == 0 else (0, 512, 1024)
            for b in range(len(edges) - 1):
                cols = slice(edges[b], edges[b + 1])
                acc = psum.tile([P, edges[b + 1] - edges[b]], F32, name="acc", tag="bank")
                nc.tensor.matmul_mx(
                    out=acc[:],
                    lhsT=w1c[:, t * P : (t + 1) * P].bitcast(FP8X4),
                    lhsT_scale=w1s[:, t * P : (t + 1) * P],
                    rhs=gw[:, cols].bitcast(FP8X4),
                    rhs_scale=gs[:, cols],
                    start=True,
                    stop=True,
                )
                if b == 2:
                    nc.vector.tensor_scalar_max(ht[:, cols], acc[:], 0.0)
                else:
                    nc.scalar.activation(ht[:, cols], acc[:], ACT.Relu)
            h.append(ht)

        nb = [sb.tile([P, PACK, V], BF16, name=f"nb{d}", align_bytes=64) for d in range(4)]
        for t in range(PACK):
            for d in range(4):
                nc.vector.tensor_copy(nb[d][:, t, :], h[t][:].indirect(pos_t[d][:]))
        m01 = sb.tile([P, PACK, V], BF16, name="m01", align_bytes=64)
        m23 = sb.tile([P, PACK, V], BF16, name="m23", align_bytes=64)
        nc.vector.tensor_tensor(m01[:], nb[0][:], nb[1][:], MAX)
        nc.vector.tensor_tensor(m23[:], nb[2][:], nb[3][:], MAX)

        def interleave(dst, src):
            nc.scalar.copy(
                dst.rearrange("p (c i t) -> p c t i", i=4, t=PACK), src[:].rearrange("p t (c i) -> p c t i", i=4)
            )

        def gather_cen(dst, t, v0, v1):
            nc.vector.tensor_copy(dst, h[t][:].indirect(cen_t[:, v0 // 16 : v1 // 16]))

        zc = sb.tile([P, V], U32, name="zc", align_bytes=64)
        zs = sb.tile([P, V], U8, name="zs", align_bytes=64)
        cc = sb.tile([P, V], U32, name="cc", align_bytes=64)
        cs = sb.tile([P, V], U8, name="cs", align_bytes=64)

        def quant(codes, scales, v0, v1, src):
            nc.vector.quantize_mx(out=codes[:, v0:v1].bitcast(FP8X4), scales=scales[:, v0:v1], in_=src[:])

        cA = sb.tile([P, PACK, 256], BF16, name="cA", tag="nb0", align_bytes=64)
        gather_cen(cA[:, 0, :], 0, 0, 256)
        zi = sb.tile([P, PACK * V], BF16, name="zi", align_bytes=64)
        for u in range(2):
            z = sb.tile([P, PACK, 256], BF16, name=f"zp{u}", align_bytes=64)
            nc.vector.tensor_tensor(z[:], m01[:, :, u * 256 : (u + 1) * 256], m23[:, :, u * 256 : (u + 1) * 256], MAX)
            interleave(zi[:, u * PACK * 256 : (u + 1) * PACK * 256], z)
        for t in range(1, PACK):
            gather_cen(cA[:, t, :], t, 0, 256)
        iA = sb.tile([P, PACK * 256], BF16, name="iA", align_bytes=64)
        interleave(iA[:], cA)
        cB = sb.tile([P, PACK, 128], BF16, name="cB", tag="nb1", align_bytes=64)
        for t in range(PACK):
            gather_cen(cB[:, t, :], t, 256, 384)
        iB = sb.tile([P, PACK * 128], BF16, name="iB", align_bytes=64)
        interleave(iB[:], cB)
        quant(zc, zs, 0, 512, zi)
        quant(cc, cs, 0, 256, iA)
        iC = sb.tile([P, PACK * 128], BF16, name="iC", tag="nb0", align_bytes=64)
        iC_v = iC[:].rearrange("p (v t) -> p t v", t=PACK)
        cC = sb.tile([P, 2, 128], BF16, name="cC", tag="zp1", align_bytes=64)
        for t in range(2):
            gather_cen(cC[:, t, :], t, 384, 512)
        nc.scalar.copy(iC[:].rearrange("p (v t) -> p v t", t=PACK)[:, :, 0:2], cC[:].rearrange("p t v -> p v t"))
        for t in range(2, PACK):
            gather_cen(iC_v[:, t, :], t, 384, 512)
        quant(cc, cs, 256, 384, iB)
        quant(cc, cs, 384, 512, iC)

        accs = [psum.tile([P, GROUP], F32, name=f"o{g}", tag="bank") for g in range(V // GROUP)]
        for g in range(V // GROUP):
            cols = slice(g * GROUP, (g + 1) * GROUP)
            nc.tensor.matmul_mx(
                out=accs[g][:], lhsT=w3w[:].bitcast(FP4X4), lhsT_scale=w3s[:],
                rhs=zc[:, cols].bitcast(FP8X4), rhs_scale=zs[:, cols], start=True, stop=False,
            )
        res = [sb.tile([P, w], F32, name=f"res{n}", align_bytes=64) for n, w in enumerate((256, 128, 128))]
        place = ((0, 0), (0, 128), (1, 0), (2, 0))
        for g in range(V // GROUP):
            cols = slice(g * GROUP, (g + 1) * GROUP)
            nc.tensor.matmul_mx(
                out=accs[g][:], lhsT=w2w[:].bitcast(FP4X4), lhsT_scale=w2s[:],
                rhs=cc[:, cols].bitcast(FP8X4), rhs_scale=cs[:, cols], start=False, stop=True,
            )
            n, c0 = place[g]
            if g == 3:
                nc.vector.tensor_copy(res[n][:, c0 : c0 + GROUP], accs[g][:])
            else:
                nc.scalar.copy(res[n][:, c0 : c0 + GROUP], accs[g][:])
            if g >= 1:
                v0 = (0, 256, 384)[n]
                queue = nc.scalar if g == 2 else nc.sync
                queue.dma_start(out[:, v0 : (g + 1) * GROUP], res[n][:])
